import numpy as np
import ml_dtypes


def mxq(x, axis, fmt="e4m3"):
    dtype, down = {"e4m3": (ml_dtypes.float8_e4m3fn, 7), "e5m2": (ml_dtypes.float8_e5m2, 14)}[fmt]
    v = np.moveaxis(np.asarray(x, np.float32).astype(ml_dtypes.bfloat16).astype(np.float64), axis, -1)
    blocks = v.reshape(v.shape[:-1] + (-1, 32))
    amax = np.abs(blocks).max(-1, keepdims=True)
    byte = np.maximum(np.where(amax > 0, np.frexp(amax)[1] - 1 + 127, 0) - down, 1)
    scale = np.exp2(byte - 127.0)
    codes = (blocks / scale).astype(np.float32).astype(dtype).astype(np.float64)
    return np.moveaxis((codes * scale).reshape(v.shape), -1, axis)


WIDE = False


def mx_kscale(k):
    if not WIDE:
        return np.ones(k)
    levels = np.array([10, -10, 5, -5, 0])
    if k % 512:
        return np.exp2(np.random.permutation(np.resize(levels, k // 32))).repeat(32)
    a = np.empty((k // 512, 16))
    for p in range(k // 512):
        a[p, :8] = np.random.permutation(np.resize(levels, 8))
        for g in range(8):
            far = levels[np.abs(levels - a[p, g]) >= 10]
            a[p, g + 8] = far[np.random.randint(len(far))]
    return np.exp2(a.ravel()).repeat(32)


def f64(x):
    return np.asarray(x).astype(np.float64)


def striped(idx):
    return np.tile(idx.reshape(-1, 16).T, (8, 1)).astype(np.uint16)


def unstriped(offs):
    return offs[:16].T.reshape(-1).astype(np.int64)


def striped8(idx):
    return np.concatenate([x.reshape(-1, 16).T for x in idx]).astype(np.uint16)


def runs(offs, k):
    lists = np.stack([offs[16 * r : 16 * r + 16].T.reshape(-1) for r in range(8)]).astype(np.int64)
    return lists[np.arange(k) % 512 // 64]


def pack_weight(w):
    k, n = w.shape
    w = f64(np.asarray(w, np.float32).astype(ml_dtypes.bfloat16)).reshape(k // 32, 32, n)
    amax = np.abs(w).max(1)
    byte = np.clip(np.where(amax > 0, np.frexp(amax)[1] - 1 + 127 - 7, 1), 1, 254)
    scaled = (w * np.exp2(127.0 - byte)[:, None, :]).reshape(k, n).astype(np.float32)
    words = np.ascontiguousarray(scaled.reshape(k // 512, 128, 4, n).transpose(0, 1, 3, 2)).astype(ml_dtypes.float8_e4m3fn).view(np.uint8)
    return words, np.ascontiguousarray(byte.astype(np.uint8).reshape(k // 512, 16, n))


def unpack_weight(words, scales):
    g, p, n, _ = words.shape
    vals = np.ascontiguousarray(words).view(ml_dtypes.float8_e4m3fn).astype(np.float64) * np.repeat(np.exp2(scales.astype(np.float64) - 127.0), 8, axis=1)[..., None]
    return vals.transpose(0, 1, 3, 2).reshape(g * 512, n)


E2M1 = np.array([0.0, 0.5, 1.0, 1.5, 2.0, 3.0, 4.0, 6.0, -0.0, -0.5, -1.0, -1.5, -2.0, -3.0, -4.0, -6.0])


def pack_fp4(w):
    k, n = w.shape
    w = f64(np.asarray(w, np.float32).astype(ml_dtypes.bfloat16)).reshape(k // 32, 32, n)
    amax = np.abs(w).max(1)
    mant, ex = np.frexp(amax / 6.0)
    byte = np.clip(np.where(amax > 0, np.where(mant > 0.5, ex, ex - 1) + 127, 1), 1, 254)
    scaled = (w * np.exp2(127.0 - byte)[:, None, :]).reshape(k, n).astype(np.float32)
    c = np.ascontiguousarray(scaled.reshape(k // 512, 128, 4, n).transpose(0, 1, 3, 2)).astype(ml_dtypes.float4_e2m1fn).view(np.uint8) & 0xF
    words = (c[..., 0::2] | (c[..., 1::2] << 4)).reshape(k // 512, 128, 2 * n)
    return np.ascontiguousarray(words), np.ascontiguousarray(byte.astype(np.uint8).reshape(k // 512, 16, n))


def unpack_fp4(words, scales):
    g, _, n = scales.shape
    words = np.ascontiguousarray(words).reshape(g, 128, n, 2)
    nib = np.empty((g, 128, n, 4), np.uint8)
    nib[..., 0::2] = words & 0xF
    nib[..., 1::2] = words >> 4
    vals = E2M1[nib] * np.repeat(np.exp2(scales.astype(np.float64) - 127.0), 8, axis=1)[..., None]
    return vals.transpose(0, 1, 3, 2).reshape(g * 512, n)


def relu(v):
    return np.maximum(v, 0.0)

def planes(y):
    n, m = y.shape
    v = y.astype(np.float32).astype(ml_dtypes.bfloat16).astype(np.float64).reshape(n // 32, 32, m)
    top = np.abs(v).max(1)
    byte = np.clip(np.where(top > 0, np.frexp(top)[1] - 1 + 127 - 7, 1), 1, 254)
    codes = (v * np.exp2(127.0 - byte)[:, None, :]).reshape(n, m).astype(np.float32).astype(ml_dtypes.float8_e4m3fn).view(np.uint8)
    words = codes.reshape(n // 512, 128, 4, m).transpose(0, 1, 3, 2)
    return np.ascontiguousarray(words), np.ascontiguousarray(byte.astype(np.uint8).reshape(n // 512, 16, m))


K, T, S, V, N, H = 512, 2048, 1024, 512, 512, 512


def setup_inputs():
    n = np.random.standard_normal
    s = mx_kscale(K)[:, None]
    u = mx_kscale(H)
    packed_xT = pack_weight(n((K, T)) * s)
    packed_w3 = pack_fp4(n((H, N)) / np.sqrt(H) / u[:, None])
    return {
        "x_words": packed_xT[0],
        "x_scales": packed_xT[1],
        "w1": (n((K, H)) / np.sqrt(K) / s * u).astype(np.float32),
        "w2": (n((H, H)) / np.sqrt(H) / u[:, None] * u).astype(np.float32),
        "res": n((N, S)).astype(np.float32),
        "w3_words": packed_w3[0],
        "w3_scales": packed_w3[1],
        "offs": striped(np.random.permutation(T)[:S]),
        "l1": striped8(np.stack([np.random.permutation(S)[:V] for _ in range(8)])),
        "r1": striped8(np.stack([np.random.permutation(S)[:V] for _ in range(8)])),
        "par": striped8(np.random.randint(0, V, (8, S))),
    }


def reference(x_words, x_scales, w1, w2, res, w3_words, w3_scales, offs, l1, r1, par):
    xq = unpack_weight(x_words, x_scales)[:, unstriped(offs)]
    y = mxq(f64(w1), 0, "e4m3").T @ xq
    z = y[np.arange(H)[:, None], runs(l1, H)] + y[np.arange(H)[:, None], runs(r1, H)]
    h = relu(mxq(f64(w2), 0, "e4m3").T @ mxq(z, 0, "e4m3"))
    z2 = h[np.arange(H)[:, None], runs(par, H)] - (0.25 * y)
    out_0 = f64(res) + (unpack_fp4(w3_words, w3_scales).T @ mxq(z2, 0, "e4m3"))
    return (out_0,) + planes(out_0)

@@ -1,0 +1,266 @@
+from contextlib import ExitStack
+
+import concourse.mybir as mybir
+
+K, T, S, V, H, N = 512, 2048, 1024, 512, 512, 512
+FLOPS = 2 * K * H * S + 2 * H * H * V + 2 * H * N * S
+
+F32 = mybir.dt.float32
+BF16 = mybir.dt.bfloat16
+I32 = mybir.dt.int32
+U32 = mybir.dt.uint32
+U16 = mybir.dt.uint16
+U8 = mybir.dt.uint8
+FP8X4 = mybir.dt.float8_e4m3fn_x4
+FP4X4 = mybir.dt.float4_e2m1fn_x4
+ADD = mybir.AluOpType.add
+SUB = mybir.AluOpType.subtract
+COPY = mybir.ActivationFunctionType.Copy
+RELU = mybir.ActivationFunctionType.Relu
+
+P = 128
+PACK = 4
+LINE = 4
+STRIPE = 16
+BANK = 512
+QUADS = 4
+
+X_CHUNK = 512
+W_CHUNK = 256
+V_CHUNK = 256
+Z_SPLIT = 176
+S_CHUNKS = (256, 256, 256, 128, 128)
+
+
+def tile_picked_inout_relu_po_kernel(
+    tc, x_words, x_scales, w1, w2, res, w3_words, w3_scales, offs, l1, r1, par, out_0, out_1, out_2
+):
+    nc = tc.nc
+    with ExitStack() as ctx:
+        lists = ctx.enter_context(tc.tile_pool(name="lists", bufs=1))
+        keep = ctx.enter_context(tc.tile_pool(name="keep", bufs=1))
+        psum = ctx.enter_context(tc.psum_pool(name="psum", bufs=8))
+
+        def held(shape, dtype, name):
+            return keep.tile(shape, dtype, name=name, align_bytes=64)
+
+        def bank(name):
+            return psum.tile([P, BANK], F32, name=name, tag="bank")
+
+        def load_list(src, name):
+            tile = lists.tile(list(src.shape), U16, name=name)
+            nc.sync.dma_start(tile[:], src)
+            return tile
+
+        def entries(list_tile, first, count):
+            return list_tile[:, first // STRIPE : (first + count) // STRIPE]
+
+        def load_scale_rows(queue, tile, rows):
+            for q in range(QUADS):
+                queue.dma_start(tile[32 * q : 32 * q + 4, :].bitcast(I32), rows[4 * q : 4 * q + 4, :].bitcast(I32))
+
+        def load_weight(w, name):
+            view = w.rearrange("(p j) c -> p j c", j=PACK)
+            pieces = []
+            for c0 in range(0, H, W_CHUNK):
+                raw = held([P, PACK, W_CHUNK], F32, "%s_raw%d" % (name, c0))
+                nc.sync.dma_start(raw[:], view[:, :, c0 : c0 + W_CHUNK])
+                pieces.append(raw)
+            return pieces
+
+        def deal_weight(copy, raw, dealt, piece):
+            m0 = piece * W_CHUNK // PACK
+            copy(
+                dealt[:, :, m0 : m0 + W_CHUNK // PACK, :].rearrange("p t m j -> p m j t"),
+                raw[:].rearrange("p j (m t) -> p m j t", t=PACK),
+            )
+
+        def scalar_copy(dst, src, scale=1.0):
+            nc.scalar.activation(dst, src, COPY, scale=scale)
+
+        def weave_views(dst, src, c0, c1):
+            return (
+                dst[:, PACK * c0 : PACK * c1].rearrange("p (c i t) -> p c t i", i=LINE, t=PACK),
+                src[:, :, c0:c1].rearrange("p t (c i) -> p c t i", i=LINE),
+            )
+
+        def weave(dst, src, scale):
+            scalar_copy(*weave_views(dst, src, 0, src.shape[2]), scale)
+
+        def quantize(codes, scales, values):
+            nc.vector.quantize_mx(out=codes.bitcast(FP8X4), scales=scales, in_=values)
+
+        xs_table = held([P, T], U8, "xs_table")
+        nc.vector.memset(xs_table[:].bitcast(I32), 0)
+        w3s_raw = held([P, N], U8, "w3s_raw")
+        nc.vector.memset(w3s_raw[:].bitcast(I32), 0)
+
+        offs_t = load_list(offs, "offs_t")
+        load_scale_rows(nc.scalar, xs_table, x_scales[0])
+        xw_table = held([P, T], U32, "xw_table")
+        nc.sync.dma_start(xw_table[:].bitcast(I32), x_words[0].rearrange("p n t -> p (n t)").bitcast(I32))
+        w1_raw = load_weight(w1, "w1")
+        l_t = load_list(l1, "l_t")
+        r_t = load_list(r1, "r_t")
+        w3w_raw = held([P, 2 * N], U8, "w3w_raw")
+        nc.sync.dma_start(w3w_raw[:].bitcast(I32), w3_words[0].bitcast(I32))
+        load_scale_rows(nc.sync, w3s_raw, w3_scales[0])
+        w2_raw = load_weight(w2, "w2")
+        par_t = load_list(par, "par_t")
+        res_view = res.rearrange("(p t) j -> p t j", t=PACK)
+        out_view = out_0.rearrange("(p t) j -> p t j", t=PACK)
+        starts = [sum(S_CHUNKS[:c]) for c in range(len(S_CHUNKS))]
+        res_t = []
+        for j0, n in zip(starts, S_CHUNKS):
+            tile = held([P, PACK, n], F32, "res%d" % j0)
+            nc.sync.dma_start(tile[:], res_view[:, :, j0 : j0 + n])
+            res_t.append(tile)
+
+        x_scale = held([P, S], U8, "x_scale")
+        nc.vector.tensor_copy(x_scale[:], xs_table[:].indirect(offs_t[:]))
+        x_code = []
+        for j0 in range(0, S, X_CHUNK):
+            tile = held([P, X_CHUNK], U32, "x_code%d" % j0)
+            nc.vector.tensor_copy(tile[:], xw_table[:].indirect(entries(offs_t, j0, X_CHUNK)))
+            x_code.append(tile)
+
+        w1_dealt = held([P, PACK, P, PACK], BF16, "w1_dealt")
+        deal_weight(scalar_copy, w1_raw[0], w1_dealt, 0)
+        deal_weight(nc.vector.tensor_copy, w1_raw[1], w1_dealt, 1)
+        w1_code = [held([P, P], U32, "w1_code%d" % t) for t in range(PACK)]
+        w1_scale = [held([P, P], U8, "w1_scale%d" % t) for t in range(PACK)]
+        for t in range(PACK):
+            quantize(w1_code[t][:], w1_scale[t][:], w1_dealt[:, t, :, :].rearrange("p m j -> p (m j)"))
+
+        y = [held([P, S], F32, "y%d" % t) for t in range(PACK)]
+        for t in range(PACK):
+            for c, j0 in enumerate(range(0, S, X_CHUNK)):
+                acc = bank("y_acc")
+                nc.tensor.matmul_mx(
+                    out=acc[:],
+                    lhsT=w1_code[t][:].bitcast(FP8X4),
+                    lhsT_scale=w1_scale[t][:],
+                    rhs=x_code[c][:].bitcast(FP8X4),
+                    rhs_scale=x_scale[:, j0 : j0 + X_CHUNK],
+                    start=True,
+                    stop=True,
+                )
+                if t == 0 and c == 1:
+                    nc.vector.tensor_copy(y[t][:, j0 : j0 + X_CHUNK], acc[:])
+                else:
+                    nc.scalar.copy(y[t][:, j0 : j0 + X_CHUNK], acc[:])
+
+        w3_code = held([P, 2 * N], U8, "w3_code")
+        nc.vector.tensor_copy(
+            w3_code[:].rearrange("p (t m b) -> p m t b", t=PACK, b=2),
+            w3w_raw[:].rearrange("p (m t b) -> p m t b", t=PACK, b=2),
+        )
+        w3_scale = held([P, N], U8, "w3_scale")
+        nc.vector.tensor_copy(
+            w3_scale[:].rearrange("p (t m) -> p m t", t=PACK),
+            w3s_raw[:].rearrange("p (m t) -> p m t", t=PACK),
+        )
+
+        w2_dealt = held([P, PACK, P, PACK], BF16, "w2_dealt")
+        for piece, raw in enumerate(w2_raw):
+            deal_weight(scalar_copy, raw, w2_dealt, piece)
+        w2_code = held([P, H], U32, "w2_code")
+        w2_scale = held([P, H], U8, "w2_scale")
+
+        h4 = [held([P, V], F32, "h4_%d" % t) for t in range(PACK)]
+        left_all = held([P, PACK * V_CHUNK], F32, "left")
+        for v0 in range(0, V, V_CHUNK):
+            turn = 2 * (v0 // V_CHUNK)
+            left = [left_all[:, (t + turn) % PACK * V_CHUNK : ((t + turn) % PACK + 1) * V_CHUNK] for t in range(PACK)]
+            z = held([P, PACK, V_CHUNK], F32, "z%d" % v0)
+            for pair in range(0, PACK, 2):
+                for t in (pair, pair + 1):
+                    nc.vector.tensor_copy(left[t], y[t][:].indirect(entries(l_t, v0, V_CHUNK)))
+                for t in (pair, pair + 1):
+                    nc.vector.tensor_tensor(z[:, t, :], y[t][:].indirect(entries(r_t, v0, V_CHUNK)), left[t], ADD)
+            if v0 == 0:
+                quantize(w2_code[:], w2_scale[:], w2_dealt[:].rearrange("p t m j -> p (t m j)"))
+            z_woven = held([P, PACK * V_CHUNK], BF16, "z_woven%d" % v0)
+            if v0 + V_CHUNK < V:
+                weave(z_woven, z, 1.0)
+            else:
+                nc.vector.tensor_copy(*weave_views(z_woven, z, 0, Z_SPLIT))
+                scalar_copy(*weave_views(z_woven, z, Z_SPLIT, V_CHUNK))
+            z_code = held([P, V_CHUNK], U32, "z_code%d" % v0)
+            z_scale = held([P, V_CHUNK], U8, "z_scale%d" % v0)
+            quantize(z_code[:], z_scale[:], z_woven[:])
+            for t in range(PACK):
+                acc = bank("h_acc")
+                nc.tensor.matmul_mx(
+                    out=acc[:, :V_CHUNK],
+                    lhsT=w2_code[:, t * P : (t + 1) * P].bitcast(FP8X4),
+                    lhsT_scale=w2_scale[:, t * P : (t + 1) * P],
+                    rhs=z_code[:].bitcast(FP8X4),
+                    rhs_scale=z_scale[:],
+                    start=True,
+                    stop=True,
+                )
+                nc.scalar.activation(h4[t][:, v0 : v0 + V_CHUNK], acc[:, :V_CHUNK], RELU, scale=4.0)
+
+        out_scale = held([P, S], U8, "out_scale")
+        words_view = out_1[0].rearrange("p n t -> p (n t)").bitcast(I32)
+        state = {}
+
+        def fetch(c):
+            j0, n = starts[c], S_CHUNKS[c]
+            z2 = keep.tile([P, PACK, n], F32, name="z2_%d" % j0, tag="z2", bufs=2, align_bytes=64)
+            for t in range(PACK):
+                nc.vector.tensor_tensor(z2[:, t, :], h4[t][:].indirect(entries(par_t, j0, n)), y[t][:, j0 : j0 + n], SUB)
+            woven = held([P, PACK * n], BF16, "z2_woven%d" % j0)
+            weave(woven, z2, 0.25)
+            state[c] = woven
+
+        def multiply(c):
+            j0, n = starts[c], S_CHUNKS[c]
+            code = held([P, n], U32, "z2_code%d" % j0)
+            scale = held([P, n], U8, "z2_scale%d" % j0)
+            quantize(code[:], scale[:], state[c][:])
+            per_bank = BANK // n
+            banks = []
+            for t0 in range(0, PACK, per_bank):
+                acc = bank("out_acc")
+                for t in range(t0, t0 + per_bank):
+                    nc.tensor.matmul_mx(
+                        out=acc[:, (t - t0) * n : (t - t0 + 1) * n],
+                        lhsT=w3_code[:, 2 * t * P : 2 * (t + 1) * P].bitcast(FP4X4),
+                        lhsT_scale=w3_scale[:, t * P : (t + 1) * P],
+                        rhs=code[:].bitcast(FP8X4),
+                        rhs_scale=scale[:],
+                        start=True,
+                        stop=True,
+                    )
+                banks.append(acc)
+            state[c] = banks
+
+        def add(c):
+            j0, n = starts[c], S_CHUNKS[c]
+            result = held([P, PACK, n], F32, "result%d" % j0)
+            flat = result[:].rearrange("p t j -> p (t j)")
+            base = res_t[c][:].rearrange("p t j -> p (t j)")
+            for b, acc in enumerate(state[c]):
+                nc.vector.tensor_tensor(flat[:, b * BANK : (b + 1) * BANK], acc[:], base[:, b * BANK : (b + 1) * BANK], ADD)
+            nc.sync.dma_start(out_view[:, :, j0 : j0 + n], result[:])
+            woven = held([P, PACK * n], BF16, "out_woven%d" % j0)
+            weave(woven, result, 1.0)
+            state[c] = woven
+
+        def hand_on(c):
+            j0, n = starts[c], S_CHUNKS[c]
+            code = held([P, n], U32, "out_code%d" % j0)
+            quantize(code[:], out_scale[:, j0 : j0 + n], state[c][:])
+            nc.sync.dma_start(words_view[:, j0 : j0 + n], code[:].bitcast(I32))
+
+        stages = (fetch, multiply, add, hand_on)
+        for step in range(len(S_CHUNKS) + len(stages) - 1):
+            for lag, stage in enumerate(stages):
+                if 0 <= step - lag < len(S_CHUNKS):
+                    stage(step - lag)
+
+        for q in range(QUADS):
+            queue = nc.scalar if q % 2 else nc.sync
+            queue.dma_start(out_2[0, 4 * q : 4 * q + 4, :].bitcast(I32), out_scale[32 * q : 32 * q + 4, :].bitcast(I32))

@@ -55,9 +55,9 @@ def tile_picked_inout_relu_po_kernel(
         def entries(list_tile, first, count):
             return list_tile[:, first // STRIPE : (first + count) // STRIPE]
 
-        def load_scale_rows(queue, tile, rows):
+        def load_scale_rows(queues, tile, rows):
             for q in range(QUADS):
-                queue.dma_start(tile[32 * q : 32 * q + 4, :].bitcast(I32), rows[4 * q : 4 * q + 4, :].bitcast(I32))
+                queues[q % len(queues)].dma_start(tile[32 * q : 32 * q + 4, :].bitcast(I32), rows[4 * q : 4 * q + 4, :].bitcast(I32))
 
         def load_weight(w, name):
             view = w.rearrange("(p j) c -> p j c", j=PACK)
@@ -68,11 +68,11 @@ def tile_picked_inout_relu_po_kernel(
                 pieces.append(raw)
             return pieces
 
-        def deal_weight(copy, raw, dealt, piece):
+        def deal_weight(raw, piece, dealt, t0, t1):
             m0 = piece * W_CHUNK // PACK
-            copy(
-                dealt[:, :, m0 : m0 + W_CHUNK // PACK, :].rearrange("p t m j -> p m j t"),
-                raw[:].rearrange("p j (m t) -> p m j t", t=PACK),
+            scalar_copy(
+                dealt[:, :, m0 : m0 + W_CHUNK // PACK, :].rearrange("p t m j -> p m t j"),
+                raw[:].rearrange("p j (m t) -> p m t j", t=PACK)[:, :, t0:t1, :],
             )
 
         def scalar_copy(dst, src, scale=1.0):
@@ -91,21 +91,22 @@ def tile_picked_inout_relu_po_kernel(
             nc.vector.quantize_mx(out=codes.bitcast(FP8X4), scales=scales, in_=values)
 
         xs_table = held([P, T], U8, "xs_table")
-        nc.vector.memset(xs_table[:].bitcast(I32), 0)
+        nc.vector.memset(xs_table[:, : T // 2].bitcast(I32), 0)
+        nc.gpsimd.memset(xs_table[:, T // 2 :].bitcast(I32), 0)
         w3s_raw = held([P, N], U8, "w3s_raw")
         nc.vector.memset(w3s_raw[:].bitcast(I32), 0)
 
         offs_t = load_list(offs, "offs_t")
-        load_scale_rows(nc.scalar, xs_table, x_scales[0])
+        l_t = load_list(l1, "l_t")
+        load_scale_rows((nc.sync, nc.scalar), xs_table, x_scales[0])
         xw_table = held([P, T], U32, "xw_table")
         nc.sync.dma_start(xw_table[:].bitcast(I32), x_words[0].rearrange("p n t -> p (n t)").bitcast(I32))
         w1_raw = load_weight(w1, "w1")
-        l_t = load_list(l1, "l_t")
         r_t = load_list(r1, "r_t")
+        w2_raw = load_weight(w2, "w2")
         w3w_raw = held([P, 2 * N], U8, "w3w_raw")
         nc.sync.dma_start(w3w_raw[:].bitcast(I32), w3_words[0].bitcast(I32))
-        load_scale_rows(nc.sync, w3s_raw, w3_scales[0])
-        w2_raw = load_weight(w2, "w2")
+        load_scale_rows((nc.sync,), w3s_raw, w3_scales[0])
         par_t = load_list(par, "par_t")
         res_view = res.rearrange("(p t) j -> p t j", t=PACK)
         out_view = out_0.rearrange("(p t) j -> p t j", t=PACK)
@@ -118,81 +119,70 @@ def tile_picked_inout_relu_po_kernel(
 
         x_scale = held([P, S], U8, "x_scale")
         nc.vector.tensor_copy(x_scale[:], xs_table[:].indirect(offs_t[:]))
-        x_code = []
+        x_code = keep.tile([P, S], U32, name="x_code", tag="after_y", align_bytes=64)
         for j0 in range(0, S, X_CHUNK):
-            tile = held([P, X_CHUNK], U32, "x_code%d" % j0)
-            nc.vector.tensor_copy(tile[:], xw_table[:].indirect(entries(offs_t, j0, X_CHUNK)))
-            x_code.append(tile)
+            nc.vector.tensor_copy(x_code[:, j0 : j0 + X_CHUNK], xw_table[:].indirect(entries(offs_t, j0, X_CHUNK)))
 
-        w1_dealt = held([P, PACK, P, PACK], BF16, "w1_dealt")
-        deal_weight(scalar_copy, w1_raw[0], w1_dealt, 0)
-        deal_weight(nc.vector.tensor_copy, w1_raw[1], w1_dealt, 1)
+        w1_first = held([P, 1, P, PACK], BF16, "w1_first")
+        w1_rest = keep.tile([P, PACK - 1, P, PACK], BF16, name="w1_rest", tag="after_rest", align_bytes=64)
+        for piece, raw in enumerate(w1_raw):
+            deal_weight(raw, piece, w1_first, 0, 1)
+            deal_weight(raw, piece, w1_rest, 1, PACK)
         w1_code = [held([P, P], U32, "w1_code%d" % t) for t in range(PACK)]
         w1_scale = [held([P, P], U8, "w1_scale%d" % t) for t in range(PACK)]
-        for t in range(PACK):
-            quantize(w1_code[t][:], w1_scale[t][:], w1_dealt[:, t, :, :].rearrange("p m j -> p (m j)"))
+        quantize(w1_code[0][:], w1_scale[0][:], w1_first[:, 0, :, :].rearrange("p m j -> p (m j)"))
+        for t in range(1, PACK):
+            quantize(w1_code[t][:], w1_scale[t][:], w1_rest[:, t - 1, :, :].rearrange("p m j -> p (m j)"))
 
         y = [held([P, S], F32, "y%d" % t) for t in range(PACK)]
         for t in range(PACK):
-            for c, j0 in enumerate(range(0, S, X_CHUNK)):
+            for j0 in range(0, S, X_CHUNK):
                 acc = bank("y_acc")
                 nc.tensor.matmul_mx(
                     out=acc[:],
                     lhsT=w1_code[t][:].bitcast(FP8X4),
                     lhsT_scale=w1_scale[t][:],
-                    rhs=x_code[c][:].bitcast(FP8X4),
+                    rhs=x_code[:, j0 : j0 + X_CHUNK].bitcast(FP8X4),
                     rhs_scale=x_scale[:, j0 : j0 + X_CHUNK],
                     start=True,
                     stop=True,
                 )
-                if t == 0 and c == 1:
-                    nc.vector.tensor_copy(y[t][:, j0 : j0 + X_CHUNK], acc[:])
-                else:
-                    nc.scalar.copy(y[t][:, j0 : j0 + X_CHUNK], acc[:])
+                nc.scalar.copy(y[t][:, j0 : j0 + X_CHUNK], acc[:])
 
-        w3_code = held([P, 2 * N], U8, "w3_code")
-        nc.vector.tensor_copy(
-            w3_code[:].rearrange("p (t m b) -> p m t b", t=PACK, b=2),
-            w3w_raw[:].rearrange("p (m t b) -> p m t b", t=PACK, b=2),
-        )
-        w3_scale = held([P, N], U8, "w3_scale")
+        w3_scale = keep.tile([P, N], U8, name="w3_scale", tag="after_rest", align_bytes=64)
         nc.vector.tensor_copy(
             w3_scale[:].rearrange("p (t m) -> p m t", t=PACK),
             w3s_raw[:].rearrange("p (m t) -> p m t", t=PACK),
         )
 
-        w2_dealt = held([P, PACK, P, PACK], BF16, "w2_dealt")
+        w2_dealt = keep.tile([P, PACK, P, PACK], BF16, name="w2_dealt", tag="after_y", align_bytes=64)
         for piece, raw in enumerate(w2_raw):
-            deal_weight(scalar_copy, raw, w2_dealt, piece)
+            deal_weight(raw, piece, w2_dealt, 0, PACK)
         w2_code = held([P, H], U32, "w2_code")
         w2_scale = held([P, H], U8, "w2_scale")
 
         h4 = [held([P, V], F32, "h4_%d" % t) for t in range(PACK)]
-        left_all = held([P, PACK * V_CHUNK], F32, "left")
-        for v0 in range(0, V, V_CHUNK):
-            turn = 2 * (v0 // V_CHUNK)
-            left = [left_all[:, (t + turn) % PACK * V_CHUNK : ((t + turn) % PACK + 1) * V_CHUNK] for t in range(PACK)]
-            z = held([P, PACK, V_CHUNK], F32, "z%d" % v0)
-            for pair in range(0, PACK, 2):
-                for t in (pair, pair + 1):
-                    nc.vector.tensor_copy(left[t], y[t][:].indirect(entries(l_t, v0, V_CHUNK)))
-                for t in (pair, pair + 1):
-                    nc.vector.tensor_tensor(z[:, t, :], y[t][:].indirect(entries(r_t, v0, V_CHUNK)), left[t], ADD)
-            if v0 == 0:
-                quantize(w2_code[:], w2_scale[:], w2_dealt[:].rearrange("p t m j -> p (t m j)"))
-            z_woven = held([P, PACK * V_CHUNK], BF16, "z_woven%d" % v0)
-            if v0 + V_CHUNK < V:
-                weave(z_woven, z, 1.0)
-            else:
-                nc.vector.tensor_copy(*weave_views(z_woven, z, 0, Z_SPLIT))
-                scalar_copy(*weave_views(z_woven, z, Z_SPLIT, V_CHUNK))
-            z_code = held([P, V_CHUNK], U32, "z_code%d" % v0)
-            z_scale = held([P, V_CHUNK], U8, "z_scale%d" % v0)
+        C = V_CHUNK
+        sums = held([P, 6 * C], F32, "sums")
+        z = [sums[:, 2 * C : 6 * C], sums[:, : 4 * C]]
+        left = [[held([P, C], F32, "left%d_%d" % (c, t))[:] for t in range(PACK - 1 + c)] for c in range(2)]
+        left[0].append(sums[:, C // 2 : C // 2 + C])
+
+        def add_right(c, t):
+            nc.vector.tensor_tensor(z[c][:, t * C : (t + 1) * C], y[t][:].indirect(entries(r_t, c * C, C)), left[c][t], ADD)
+
+        def hidden(c, split, z_woven):
+            planes = z[c].rearrange("p (t c) -> p t c", t=PACK)
+            if split:
+                nc.vector.tensor_copy(*weave_views(z_woven, planes, 0, split))
+            scalar_copy(*weave_views(z_woven, planes, split, C))
+            z_code = held([P, C], U32, "z_code%d" % c)
+            z_scale = held([P, C], U8, "z_scale%d" % c)
             quantize(z_code[:], z_scale[:], z_woven[:])
             for t in range(PACK):
                 acc = bank("h_acc")
                 nc.tensor.matmul_mx(
-                    out=acc[:, :V_CHUNK],
+                    out=acc[:, :C],
                     lhsT=w2_code[:, t * P : (t + 1) * P].bitcast(FP8X4),
                     lhsT_scale=w2_scale[:, t * P : (t + 1) * P],
                     rhs=z_code[:].bitcast(FP8X4),
@@ -200,7 +190,25 @@ def tile_picked_inout_relu_po_kernel(
                     start=True,
                     stop=True,
                 )
-                nc.scalar.activation(h4[t][:, v0 : v0 + V_CHUNK], acc[:, :V_CHUNK], RELU, scale=4.0)
+                nc.scalar.activation(h4[t][:, c * C : (c + 1) * C], acc[:, :C], RELU, scale=4.0)
+
+        for t in range(PACK):
+            for c in range(2):
+                nc.vector.tensor_copy(left[c][t], y[t][:].indirect(entries(l_t, c * C, C)))
+            add_right(0, t)
+        add_right(1, 0)
+        add_right(1, 1)
+        quantize(w2_code[:], w2_scale[:], w2_dealt[:].rearrange("p t m j -> p (t m j)"))
+        hidden(0, 0, held([P, PACK * C], BF16, "z_woven0"))
+        add_right(1, 2)
+        add_right(1, 3)
+        hidden(1, Z_SPLIT, keep.tile([P, PACK * C], BF16, name="z_woven1", tag="after_z", align_bytes=64))
+
+        w3_code = keep.tile([P, 2 * N], U8, name="w3_code", tag="after_z", align_bytes=64)
+        nc.vector.tensor_copy(
+            w3_code[:].rearrange("p (t m b) -> p m t b", t=PACK, b=2),
+            w3w_raw[:].rearrange("p (m t b) -> p m t b", t=PACK, b=2),
+        )
 
         out_scale = held([P, S], U8, "out_scale")
         words_view = out_1[0].rearrange("p n t -> p (n t)").bitcast(I32)

@@ -97,11 +97,11 @@ def tile_picked_inout_relu_po_kernel(
         nc.vector.memset(w3s_raw[:].bitcast(I32), 0)
 
         offs_t = load_list(offs, "offs_t")
-        l_t = load_list(l1, "l_t")
         load_scale_rows((nc.sync, nc.scalar), xs_table, x_scales[0])
         xw_table = held([P, T], U32, "xw_table")
         nc.sync.dma_start(xw_table[:].bitcast(I32), x_words[0].rearrange("p n t -> p (n t)").bitcast(I32))
         w1_raw = load_weight(w1, "w1")
+        l_t = load_list(l1, "l_t")
         r_t = load_list(r1, "r_t")
         w2_raw = load_weight(w2, "w2")
         w3w_raw = held([P, 2 * N], U8, "w3w_raw")
@@ -124,7 +124,7 @@ def tile_picked_inout_relu_po_kernel(
             nc.vector.tensor_copy(x_code[:, j0 : j0 + X_CHUNK], xw_table[:].indirect(entries(offs_t, j0, X_CHUNK)))
 
         w1_first = held([P, 1, P, PACK], BF16, "w1_first")
-        w1_rest = keep.tile([P, PACK - 1, P, PACK], BF16, name="w1_rest", tag="after_rest", align_bytes=64)
+        w1_rest = held([P, PACK - 1, P, PACK], BF16, "w1_rest")
         for piece, raw in enumerate(w1_raw):
             deal_weight(raw, piece, w1_first, 0, 1)
             deal_weight(raw, piece, w1_rest, 1, PACK)
@@ -148,12 +148,6 @@ def tile_picked_inout_relu_po_kernel(
                     stop=True,
                 )
                 nc.scalar.copy(y[t][:, j0 : j0 + X_CHUNK], acc[:])
-
-        w3_scale = keep.tile([P, N], U8, name="w3_scale", tag="after_rest", align_bytes=64)
-        nc.vector.tensor_copy(
-            w3_scale[:].rearrange("p (t m) -> p m t", t=PACK),
-            w3s_raw[:].rearrange("p (m t) -> p m t", t=PACK),
-        )
 
         w2_dealt = keep.tile([P, PACK, P, PACK], BF16, name="w2_dealt", tag="after_y", align_bytes=64)
         for piece, raw in enumerate(w2_raw):
@@ -204,10 +198,16 @@ def tile_picked_inout_relu_po_kernel(
         add_right(1, 3)
         hidden(1, Z_SPLIT, keep.tile([P, PACK * C], BF16, name="z_woven1", tag="after_z", align_bytes=64))
 
-        w3_code = keep.tile([P, 2 * N], U8, name="w3_code", tag="after_z", align_bytes=64)
+        w3_dealt = keep.tile([P, 3 * N], U8, name="w3_dealt", tag="after_z", align_bytes=64)
+        w3_code = w3_dealt[:, : 2 * N]
+        w3_scale = w3_dealt[:, 2 * N :]
         nc.vector.tensor_copy(
-            w3_code[:].rearrange("p (t m b) -> p m t b", t=PACK, b=2),
-            w3w_raw[:].rearrange("p (m t b) -> p m t b", t=PACK, b=2),
+            w3_scale.rearrange("p (t m) -> p t m", t=PACK),
+            w3s_raw[:].rearrange("p (m t) -> p t m", t=PACK),
+        )
+        nc.vector.tensor_copy(
+            w3_code.rearrange("p (t m b) -> p t m b", t=PACK, b=2),
+            w3w_raw[:].rearrange("p (m t b) -> p t m b", t=PACK, b=2),
         )
 
         out_scale = held([P, S], U8, "out_scale")

from contextlib import ExitStack

import concourse.mybir as mybir

K, T, S, V, H, N = 512, 2048, 1024, 512, 512, 512
FLOPS = 2 * K * H * S + 2 * H * H * V + 2 * H * N * S

F32 = mybir.dt.float32
BF16 = mybir.dt.bfloat16
I32 = mybir.dt.int32
U32 = mybir.dt.uint32
U16 = mybir.dt.uint16
U8 = mybir.dt.uint8
FP8X4 = mybir.dt.float8_e4m3fn_x4
FP4X4 = mybir.dt.float4_e2m1fn_x4
ADD = mybir.AluOpType.add
SUB = mybir.AluOpType.subtract
COPY = mybir.ActivationFunctionType.Copy
RELU = mybir.ActivationFunctionType.Relu

P = 128
PACK = 4
LINE = 4
STRIPE = 16
BANK = 512
QUADS = 4

X_CHUNK = 512
W_CHUNK = 256
V_CHUNK = 256
Z_SPLIT = 176
S_CHUNKS = (256, 256, 256, 128, 128)


def tile_picked_inout_relu_po_kernel(
    tc, x_words, x_scales, w1, w2, res, w3_words, w3_scales, offs, l1, r1, par, out_0, out_1, out_2
):
    nc = tc.nc
    with ExitStack() as ctx:
        lists = ctx.enter_context(tc.tile_pool(name="lists", bufs=1))
        keep = ctx.enter_context(tc.tile_pool(name="keep", bufs=1))
        psum = ctx.enter_context(tc.psum_pool(name="psum", bufs=8))

        def held(shape, dtype, name):
            return keep.tile(shape, dtype, name=name, align_bytes=64)

        def bank(name):
            return psum.tile([P, BANK], F32, name=name, tag="bank")

        def load_list(src, name):
            tile = lists.tile(list(src.shape), U16, name=name)
            nc.sync.dma_start(tile[:], src)
            return tile

        def entries(list_tile, first, count):
            return list_tile[:, first // STRIPE : (first + count) // STRIPE]

        def load_scale_rows(queues, tile, rows):
            for q in range(QUADS):
                queues[q % len(queues)].dma_start(tile[32 * q : 32 * q + 4, :].bitcast(I32), rows[4 * q : 4 * q + 4, :].bitcast(I32))

        def load_weight(w, name):
            view = w.rearrange("(p j) c -> p j c", j=PACK)
            pieces = []
            for c0 in range(0, H, W_CHUNK):
                raw = held([P, PACK, W_CHUNK], F32, "%s_raw%d" % (name, c0))
                nc.sync.dma_start(raw[:], view[:, :, c0 : c0 + W_CHUNK])
                pieces.append(raw)
            return pieces

        def deal_weight(raw, piece, dealt, t0, t1):
            m0 = piece * W_CHUNK // PACK
            scalar_copy(
                dealt[:, :, m0 : m0 + W_CHUNK // PACK, :].rearrange("p t m j -> p m t j"),
                raw[:].rearrange("p j (m t) -> p m t j", t=PACK)[:, :, t0:t1, :],
            )

        def scalar_copy(dst, src, scale=1.0):
            nc.scalar.activation(dst, src, COPY, scale=scale)

        def weave_views(dst, src, c0, c1):
            return (
                dst[:, PACK * c0 : PACK * c1].rearrange("p (c i t) -> p c t i", i=LINE, t=PACK),
                src[:, :, c0:c1].rearrange("p t (c i) -> p c t i", i=LINE),
            )

        def weave(dst, src, scale):
            scalar_copy(*weave_views(dst, src, 0, src.shape[2]), scale)

        def quantize(codes, scales, values):
            nc.vector.quantize_mx(out=codes.bitcast(FP8X4), scales=scales, in_=values)

        xs_table = held([P, T], U8, "xs_table")
        nc.vector.memset(xs_table[:, : T // 2].bitcast(I32), 0)
        nc.gpsimd.memset(xs_table[:, T // 2 :].bitcast(I32), 0)
        w3s_raw = held([P, N], U8, "w3s_raw")
        nc.vector.memset(w3s_raw[:].bitcast(I32), 0)

        offs_t = load_list(offs, "offs_t")
        load_scale_rows((nc.sync, nc.scalar), xs_table, x_scales[0])
        xw_table = held([P, T], U32, "xw_table")
        nc.sync.dma_start(xw_table[:].bitcast(I32), x_words[0].rearrange("p n t -> p (n t)").bitcast(I32))
        w1_raw = load_weight(w1, "w1")
        l_t = load_list(l1, "l_t")
        r_t = load_list(r1, "r_t")
        w2_raw = load_weight(w2, "w2")
        w3w_raw = held([P, 2 * N], U8, "w3w_raw")
        nc.sync.dma_start(w3w_raw[:].bitcast(I32), w3_words[0].bitcast(I32))
        load_scale_rows((nc.sync,), w3s_raw, w3_scales[0])
        par_t = load_list(par, "par_t")
        res_view = res.rearrange("(p t) j -> p t j", t=PACK)
        out_view = out_0.rearrange("(p t) j -> p t j", t=PACK)
        starts = [sum(S_CHUNKS[:c]) for c in range(len(S_CHUNKS))]
        res_t = []
        for j0, n in zip(starts, S_CHUNKS):
            tile = held([P, PACK, n], F32, "res%d" % j0)
            nc.sync.dma_start(tile[:], res_view[:, :, j0 : j0 + n])
            res_t.append(tile)

        x_scale = held([P, S], U8, "x_scale")
        nc.vector.tensor_copy(x_scale[:], xs_table[:].indirect(offs_t[:]))
        x_code = keep.tile([P, S], U32, name="x_code", tag="after_y", align_bytes=64)
        for j0 in range(0, S, X_CHUNK):
            nc.vector.tensor_copy(x_code[:, j0 : j0 + X_CHUNK], xw_table[:].indirect(entries(offs_t, j0, X_CHUNK)))

        w1_first = held([P, 1, P, PACK], BF16, "w1_first")
        w1_rest = held([P, PACK - 1, P, PACK], BF16, "w1_rest")
        for piece, raw in enumerate(w1_raw):
            deal_weight(raw, piece, w1_first, 0, 1)
            deal_weight(raw, piece, w1_rest, 1, PACK)
        w1_code = [held([P, P], U32, "w1_code%d" % t) for t in range(PACK)]
        w1_scale = [held([P, P], U8, "w1_scale%d" % t) for t in range(PACK)]
        quantize(w1_code[0][:], w1_scale[0][:], w1_first[:, 0, :, :].rearrange("p m j -> p (m j)"))
        for t in range(1, PACK):
            quantize(w1_code[t][:], w1_scale[t][:], w1_rest[:, t - 1, :, :].rearrange("p m j -> p (m j)"))

        y = [held([P, S], F32, "y%d" % t) for t in range(PACK)]
        for t in range(PACK):
            for j0 in range(0, S, X_CHUNK):
                acc = bank("y_acc")
                nc.tensor.matmul_mx(
                    out=acc[:],
                    lhsT=w1_code[t][:].bitcast(FP8X4),
                    lhsT_scale=w1_scale[t][:],
                    rhs=x_code[:, j0 : j0 + X_CHUNK].bitcast(FP8X4),
                    rhs_scale=x_scale[:, j0 : j0 + X_CHUNK],
                    start=True,
                    stop=True,
                )
                nc.scalar.copy(y[t][:, j0 : j0 + X_CHUNK], acc[:])

        w2_dealt = keep.tile([P, PACK, P, PACK], BF16, name="w2_dealt", tag="after_y", align_bytes=64)
        for piece, raw in enumerate(w2_raw):
            deal_weight(raw, piece, w2_dealt, 0, PACK)
        w2_code = held([P, H], U32, "w2_code")
        w2_scale = held([P, H], U8, "w2_scale")

        h4 = [held([P, V], F32, "h4_%d" % t) for t in range(PACK)]
        C = V_CHUNK
        sums = held([P, 6 * C], F32, "sums")
        z = [sums[:, 2 * C : 6 * C], sums[:, : 4 * C]]
        left = [[held([P, C], F32, "left%d_%d" % (c, t))[:] for t in range(PACK - 1 + c)] for c in range(2)]
        left[0].append(sums[:, C // 2 : C // 2 + C])

        def add_right(c, t):
            nc.vector.tensor_tensor(z[c][:, t * C : (t + 1) * C], y[t][:].indirect(entries(r_t, c * C, C)), left[c][t], ADD)

        def hidden(c, split, z_woven):
            planes = z[c].rearrange("p (t c) -> p t c", t=PACK)
            if split:
                nc.vector.tensor_copy(*weave_views(z_woven, planes, 0, split))
            scalar_copy(*weave_views(z_woven, planes, split, C))
            z_code = held([P, C], U32, "z_code%d" % c)
            z_scale = held([P, C], U8, "z_scale%d" % c)
            quantize(z_code[:], z_scale[:], z_woven[:])
            for t in range(PACK):
                acc = bank("h_acc")
                nc.tensor.matmul_mx(
                    out=acc[:, :C],
                    lhsT=w2_code[:, t * P : (t + 1) * P].bitcast(FP8X4),
                    lhsT_scale=w2_scale[:, t * P : (t + 1) * P],
                    rhs=z_code[:].bitcast(FP8X4),
                    rhs_scale=z_scale[:],
                    start=True,
                    stop=True,
                )
                nc.scalar.activation(h4[t][:, c * C : (c + 1) * C], acc[:, :C], RELU, scale=4.0)

        for t in range(PACK):
            for c in range(2):
                nc.vector.tensor_copy(left[c][t], y[t][:].indirect(entries(l_t, c * C, C)))
            add_right(0, t)
        add_right(1, 0)
        add_right(1, 1)
        quantize(w2_code[:], w2_scale[:], w2_dealt[:].rearrange("p t m j -> p (t m j)"))
        hidden(0, 0, held([P, PACK * C], BF16, "z_woven0"))
        add_right(1, 2)
        add_right(1, 3)
        hidden(1, Z_SPLIT, keep.tile([P, PACK * C], BF16, name="z_woven1", tag="after_z", align_bytes=64))

        w3_dealt = keep.tile([P, 3 * N], U8, name="w3_dealt", tag="after_z", align_bytes=64)
        w3_code = w3_dealt[:, : 2 * N]
        w3_scale = w3_dealt[:, 2 * N :]
        nc.vector.tensor_copy(
            w3_scale.rearrange("p (t m) -> p t m", t=PACK),
            w3s_raw[:].rearrange("p (m t) -> p t m", t=PACK),
        )
        nc.vector.tensor_copy(
            w3_code.rearrange("p (t m b) -> p t m b", t=PACK, b=2),
            w3w_raw[:].rearrange("p (m t b) -> p t m b", t=PACK, b=2),
        )

        out_scale = held([P, S], U8, "out_scale")
        words_view = out_1[0].rearrange("p n t -> p (n t)").bitcast(I32)
        state = {}

        def fetch(c):
            j0, n = starts[c], S_CHUNKS[c]
            z2 = keep.tile([P, PACK, n], F32, name="z2_%d" % j0, tag="z2", bufs=2, align_bytes=64)
            for t in range(PACK):
                nc.vector.tensor_tensor(z2[:, t, :], h4[t][:].indirect(entries(par_t, j0, n)), y[t][:, j0 : j0 + n], SUB)
            woven = held([P, PACK * n], BF16, "z2_woven%d" % j0)
            weave(woven, z2, 0.25)
            state[c] = woven

        def multiply(c):
            j0, n = starts[c], S_CHUNKS[c]
            code = held([P, n], U32, "z2_code%d" % j0)
            scale = held([P, n], U8, "z2_scale%d" % j0)
            quantize(code[:], scale[:], state[c][:])
            per_bank = BANK // n
            banks = []
            for t0 in range(0, PACK, per_bank):
                acc = bank("out_acc")
                for t in range(t0, t0 + per_bank):
                    nc.tensor.matmul_mx(
                        out=acc[:, (t - t0) * n : (t - t0 + 1) * n],
                        lhsT=w3_code[:, 2 * t * P : 2 * (t + 1) * P].bitcast(FP4X4),
                        lhsT_scale=w3_scale[:, t * P : (t + 1) * P],
                        rhs=code[:].bitcast(FP8X4),
                        rhs_scale=scale[:],
                        start=True,
                        stop=True,
                    )
                banks.append(acc)
            state[c] = banks

        def add(c):
            j0, n = starts[c], S_CHUNKS[c]
            result = held([P, PACK, n], F32, "result%d" % j0)
            flat = result[:].rearrange("p t j -> p (t j)")
            base = res_t[c][:].rearrange("p t j -> p (t j)")
            for b, acc in enumerate(state[c]):
                nc.vector.tensor_tensor(flat[:, b * BANK : (b + 1) * BANK], acc[:], base[:, b * BANK : (b + 1) * BANK], ADD)
            nc.sync.dma_start(out_view[:, :, j0 : j0 + n], result[:])
            woven = held([P, PACK * n], BF16, "out_woven%d" % j0)
            weave(woven, result, 1.0)
            state[c] = woven

        def hand_on(c):
            j0, n = starts[c], S_CHUNKS[c]
            code = held([P, n], U32, "out_code%d" % j0)
            quantize(code[:], out_scale[:, j0 : j0 + n], state[c][:])
            nc.sync.dma_start(words_view[:, j0 : j0 + n], code[:].bitcast(I32))

        stages = (fetch, multiply, add, hand_on)
        for step in range(len(S_CHUNKS) + len(stages) - 1):
            for lag, stage in enumerate(stages):
                if 0 <= step - lag < len(S_CHUNKS):
                    stage(step - lag)

        for q in range(QUADS):
            queue = nc.scalar if q % 2 else nc.sync
            queue.dma_start(out_2[0, 4 * q : 4 * q + 4, :].bitcast(I32), out_scale[32 * q : 32 * q + 4, :].bitcast(I32))
